import numpy as np
import ml_dtypes


def mxq(x, axis, fmt="e4m3"):
    dtype, down = {"e4m3": (ml_dtypes.float8_e4m3fn, 7), "e5m2": (ml_dtypes.float8_e5m2, 14)}[fmt]
    v = np.moveaxis(np.asarray(x, np.float32).astype(ml_dtypes.bfloat16).astype(np.float64), axis, -1)
    blocks = v.reshape(v.shape[:-1] + (-1, 32))
    amax = np.abs(blocks).max(-1, keepdims=True)
    byte = np.maximum(np.where(amax > 0, np.frexp(amax)[1] - 1 + 127, 0) - down, 1)
    scale = np.exp2(byte - 127.0)
    codes = (blocks / scale).astype(np.float32).astype(dtype).astype(np.float64)
    return np.moveaxis((codes * scale).reshape(v.shape), -1, axis)


WIDE = False


def mx_kscale(k):
    if not WIDE:
        return np.ones(k)
    levels = np.array([10, -10, 5, -5, 0])
    if k % 512:
        return np.exp2(np.random.permutation(np.resize(levels, k // 32))).repeat(32)
    a = np.empty((k // 512, 16))
    for p in range(k // 512):
        a[p, :8] = np.random.permutation(np.resize(levels, 8))
        for g in range(8):
            far = levels[np.abs(levels - a[p, g]) >= 10]
            a[p, g + 8] = far[np.random.randint(len(far))]
    return np.exp2(a.ravel()).repeat(32)


def f64(x):
    return np.asarray(x).astype(np.float64)


def striped(idx):
    return np.tile(idx.reshape(-1, 16).T, (8, 1)).astype(np.uint16)


def unstriped(offs):
    return offs[:16].T.reshape(-1).astype(np.int64)


E2M1 = np.array([0.0, 0.5, 1.0, 1.5, 2.0, 3.0, 4.0, 6.0, -0.0, -0.5, -1.0, -1.5, -2.0, -3.0, -4.0, -6.0])


def pack_weight(w, fmt):
    k, n = w.shape
    w = f64(np.asarray(w, np.float32).astype(ml_dtypes.bfloat16)).reshape(k // 32, 32, n)
    amax = np.abs(w).max(1)
    if fmt == "e4m3":
        byte = np.frexp(amax)[1] - 1 + 127 - 7
    else:
        mant, ex = np.frexp(amax / 6.0)
        byte = np.where(mant > 0.5, ex, ex - 1) + 127
    byte = np.clip(np.where(amax > 0, byte, 1), 1, 254)
    scaled = (w * np.exp2(127.0 - byte)[:, None, :]).reshape(k, n).astype(np.float32)
    by_word = np.ascontiguousarray(scaled.reshape(k // 512, 128, 4, n).transpose(0, 1, 3, 2))
    if fmt == "e4m3":
        words = by_word.astype(ml_dtypes.float8_e4m3fn).view(np.uint8)
    else:
        c = by_word.astype(ml_dtypes.float4_e2m1fn).view(np.uint8) & 0xF
        words = (c[..., 0::2] | (c[..., 1::2] << 4)).reshape(k // 512, 128, 2 * n)
    return np.ascontiguousarray(words), np.ascontiguousarray(byte.astype(np.uint8).reshape(k // 512, 16, n))


def unpack_weight(words, scales, fmt):
    g, _, n = scales.shape
    words = np.ascontiguousarray(words).reshape(g, 128, n, -1)
    if fmt == "e4m3":
        vals = words.view(ml_dtypes.float8_e4m3fn).astype(np.float64)
    else:
        nib = np.empty((g, 128, n, 4), np.uint8)
        nib[..., 0::2] = words & 0xF
        nib[..., 1::2] = words >> 4
        vals = E2M1[nib]
    vals = vals * np.repeat(np.exp2(scales.astype(np.float64) - 127.0), 8, axis=1)[..., None]
    return vals.transpose(0, 1, 3, 2).reshape(g * 512, n)


def sigmoid(v):
    return 1.0 / (1.0 + np.exp(-np.maximum(v, -700.0)))


K, T, E, C, H, N = 512, 512, 8, 128, 512, 256


def by_expert(wq, xq):
    return np.concatenate([wq[e].T @ xq[:, e * C:(e + 1) * C] for e in range(E)], axis=1)


def setup_inputs():
    n = np.random.standard_normal
    s = mx_kscale(K)[:, None]
    u = mx_kscale(H)
    first = np.random.permutation(np.repeat(np.arange(E), T // E))
    second = (first + 1 + np.random.permutation(np.repeat(np.arange(E - 1), -(-T // (E - 1)))[:T])) % E
    while np.bincount(second, minlength=E).max() != T // E:
        load = np.bincount(second, minlength=E); hi, lo = int(load.argmax()), int(load.argmin())
        t = np.flatnonzero((second == hi) & (first != lo))[0]; second[t] = lo
    slot_token = np.empty(E * C, np.int64); pos = np.empty((2, T), np.int64); fill = np.zeros(E, np.int64)
    place = np.stack([np.random.permutation(C) for _ in range(E)])
    for r, deal in enumerate((first, second)):
        for t in np.random.permutation(T):
            e = deal[t]; j = e * C + place[e, fill[e]]; fill[e] += 1; slot_token[j] = t; pos[r, t] = j
    g = np.random.uniform(0.2, 0.8, T)
    w1 = [pack_weight(m, "e2m1") for m in n((E, K, H)) / np.sqrt(K) / s[None]]
    w3 = [pack_weight(m, "e2m1") for m in n((E, K, H)) / np.sqrt(K) / s[None] * u[None, None, :]]
    w2 = [pack_weight(m, "e2m1") for m in n((E, H, N)) / np.sqrt(H) / u[None, :, None]]
    x = pack_weight(n((K, T)) * s, "e4m3")
    return {
        "x_words": x[0],
        "x_scales": x[1],
        "w1_words": np.stack([m[0] for m in w1]),
        "w1_scales": np.stack([m[1] for m in w1]),
        "w3_words": np.stack([m[0] for m in w3]),
        "w3_scales": np.stack([m[1] for m in w3]),
        "w2_words": np.stack([m[0] for m in w2]),
        "w2_scales": np.stack([m[1] for m in w2]),
        "gate": np.stack([np.tile(g, (N, 1)), np.tile(1.0 - g, (N, 1))]).astype(np.float32),
        "offs": striped(slot_token),
        "pos1": striped(pos[0]),
        "pos2": striped(pos[1]),
    }


def reference(x_words, x_scales, w1_words, w1_scales, w3_words, w3_scales, w2_words, w2_scales, gate, offs, pos1, pos2):
    idx = unstriped(offs)
    w1 = np.stack([unpack_weight(w1_words[e], w1_scales[e], "e2m1") for e in range(E)])
    w3 = np.stack([unpack_weight(w3_words[e], w3_scales[e], "e2m1") for e in range(E)])
    w2 = np.stack([unpack_weight(w2_words[e], w2_scales[e], "e2m1") for e in range(E)])
    xq = unpack_weight(x_words, x_scales, "e4m3")[:, idx]
    h = sigmoid(by_expert(w1, xq))
    h = h * by_expert(w3, xq)
    y = by_expert(w2, mxq(h, 0, "e4m3"))
    return f64(gate[0]) * y[:, unstriped(pos1)] + f64(gate[1]) * y[:, unstriped(pos2)]

@@ -1,0 +1,211 @@
+from contextlib import ExitStack
+
+import concourse.mybir as mybir
+from concourse.masks import make_identity
+
+K, T, E, C, H, N = 512, 512, 8, 128, 512, 256
+S = E * C
+FLOPS = 2 * S * (2 * K * H + H * N)
+
+F32 = mybir.dt.float32
+BF16 = mybir.dt.bfloat16
+I32 = mybir.dt.int32
+U32 = mybir.dt.uint32
+U16 = mybir.dt.uint16
+U8 = mybir.dt.uint8
+FP8X4 = mybir.dt.float8_e4m3fn_x4
+FP4X4 = mybir.dt.float4_e2m1fn_x4
+SIGMOID = mybir.ActivationFunctionType.Sigmoid
+MULT = mybir.AluOpType.mult
+ADD = mybir.AluOpType.add
+
+P = 128
+WORD_PIECES = ((0, 3), (3, 6), (6, 8))
+SCALE_PIECES = ((0, 2), (2, 5), (5, 8))
+FIRST_CHUNKS = ((0, 3), (3, 5), (5, 8))
+SECOND_CHUNKS = ((0, 4), (4, 8))
+SECOND_GROUPS = ((0, 2), (2, 4), (4, 6), (6, 7), (7, 8))
+Y_BANKS = ((0, 4), (4, 7), (7, 8))
+
+
+def load_scale_rows(queue, plane, rows):
+    by_r = rows.rearrange("e (q r) n -> r q e n", r=4)
+    for r in range(4):
+        queue.dma_start(out=plane[r:P:32].bitcast(I32), in_=by_r[r].bitcast(I32))
+
+
+def tile_moe_pkd_glu_sigmoid_kernel(
+    tc, x_words, x_scales, w1_words, w1_scales, w3_words, w3_scales, w2_words, w2_scales, gate, offs, pos1, pos2, out
+):
+    nc = tc.nc
+    with ExitStack() as ctx:
+        keep = ctx.enter_context(tc.tile_pool(name="keep", bufs=1))
+        ring = ctx.enter_context(tc.tile_pool(name="ring", bufs=2))
+        psum = ctx.enter_context(tc.psum_pool(name="psum", bufs=2))
+
+        offs_sb = keep.tile([P, S // 16], U16, name="offs_sb")
+        pos_sb = [keep.tile([P, T // 16], U16, name=f"pos_sb{j}") for j in range(2)]
+        xw = keep.tile([P, T], U32, name="xw", align_bytes=64)
+        xs = keep.tile([P, 1, T], U8, name="xs", align_bytes=64)
+        w1s = keep.tile([P, E, H], U8, name="w1s", align_bytes=64)
+        w3s = keep.tile([P, E, H], U8, name="w3s", align_bytes=64)
+        w2s = keep.tile([P, E, N], U8, name="w2s", align_bytes=64)
+        w1w = {a: keep.tile([P, b - a, 2 * H], U8, name=f"w1w{a}", align_bytes=64) for a, b in FIRST_CHUNKS}
+        w3w = {a: keep.tile([P, b - a, 2 * H], U8, name=f"w3w{a}", align_bytes=64) for a, b in FIRST_CHUNKS}
+        w2w = {a: keep.tile([P, b - a, 2 * N], U8, name=f"w2w{a}", align_bytes=64) for a, b in SECOND_CHUNKS}
+        gate_sb = [keep.tile([P, T], F32, name=f"gate_sb{j}") for j in range(2)]
+        ident = keep.tile([P, P], F32, name="ident")
+        y = [keep.tile([P, S], F32, name=f"y{m}") for m in range(2)]
+
+        for plane in (w1s, xs, w3s):
+            nc.vector.memset(plane[:].bitcast(I32), 0)
+        nc.gpsimd.memset(w2s[:].bitcast(I32), 0)
+        load_scale_rows(nc.gpsimd, w2s, w2_scales[:, 0])
+        make_identity(nc, ident[:])
+
+        def load_words(tiles, words, chunk):
+            src = words[chunk[0] : chunk[1], 0].rearrange("e p b -> p e b")
+            nc.sync.dma_start(out=tiles[chunk[0]][:].bitcast(I32), in_=src.bitcast(I32))
+
+        def expert_words(tiles, chunks, e):
+            first = [a for a, b in chunks if a <= e < b][0]
+            return tiles[first][:, e - first, :]
+
+        nc.sync.dma_start(out=xw[:].bitcast(I32), in_=x_words[0].rearrange("p t r -> p (t r)").bitcast(I32))
+        nc.sync.dma_start(offs_sb[:], offs)
+        load_scale_rows(nc.sync, w1s, w1_scales[:, 0])
+        load_words(w1w, w1_words, FIRST_CHUNKS[0])
+        load_scale_rows(nc.sync, xs, x_scales)
+        load_words(w3w, w3_words, FIRST_CHUNKS[0])
+        load_scale_rows(nc.sync, w3s, w3_scales[:, 0])
+        load_words(w1w, w1_words, FIRST_CHUNKS[1])
+        load_words(w3w, w3_words, FIRST_CHUNKS[1])
+        load_words(w2w, w2_words, SECOND_CHUNKS[0])
+        load_words(w1w, w1_words, FIRST_CHUNKS[2])
+        load_words(w3w, w3_words, FIRST_CHUNKS[2])
+        load_words(w2w, w2_words, SECOND_CHUNKS[1])
+        nc.sync.dma_start(pos_sb[0][:], pos1)
+        nc.sync.dma_start(pos_sb[1][:], pos2)
+        for j in range(2):
+            nc.sync.dma_start(out=gate_sb[j][:], in_=gate[j, 0:P, :])
+
+        slot_words = {}
+        slot_scales = {}
+        h = {}
+        hq = {}
+
+        def gather(window, dtype, pieces, found, label):
+            for first, last in pieces:
+                entries = offs_sb[:, first * C // 16 : last * C // 16]
+                got = keep.tile([P, (last - first) * C], dtype, name=f"{label}{first}", align_bytes=64)
+                nc.vector.tensor_copy(got[:], window.indirect(entries))
+                for e in range(first, last):
+                    found[e] = got[:, (e - first) * C : (e - first + 1) * C]
+
+        def first_layer(e):
+            a = psum.tile([P, H], F32, name="a")
+            b = psum.tile([P, H], F32, name="b")
+            for acc, words, scales in ((a, w1w, w1s), (b, w3w, w3s)):
+                nc.tensor.matmul_mx(
+                    out=acc[:],
+                    lhsT=slot_words[e].bitcast(FP8X4),
+                    lhsT_scale=slot_scales[e],
+                    rhs=expert_words(words, FIRST_CHUNKS, e).bitcast(FP4X4),
+                    rhs_scale=scales[:, e, :],
+                    start=True,
+                    stop=True,
+                )
+            sig = ring.tile([P, H], F32, name="sig", bufs=E)
+            h[e] = ring.tile([P, H], BF16, name="h", bufs=4)
+            nc.scalar.activation(
+                out=sig[:].rearrange("c (u p d) -> c u p d", u=2, d=2),
+                in_=a[:].rearrange("c (p u d) -> c u p d", u=2, d=2),
+                func=SIGMOID,
+            )
+            nc.vector.tensor_tensor(
+                out=h[e][:].rearrange("c (u p d) -> c u p d", u=2, d=2),
+                in0=b[:].rearrange("c (p u d) -> c u p d", u=2, d=2),
+                in1=sig[:].rearrange("c (u p d) -> c u p d", u=2, d=2),
+                op=MULT,
+            )
+
+        def turn_and_quantize(first, last):
+            n = last - first
+            turned = psum.tile([P, n, 2, C], F32, name="turned")
+            for e in range(first, last):
+                pairs = h[e][:].bitcast(F32)
+                for u in range(2):
+                    nc.tensor.transpose(turned[:, e - first, u, :], pairs[:, u * P : (u + 1) * P], ident[:])
+            grouped = ring.tile([P, n * C * 4], BF16, name="grouped", align_bytes=64)
+            nc.scalar.copy(
+                out=grouped[:].bitcast(F32).rearrange("p (e c u) -> p e c u", e=n, u=2),
+                in_=turned[:].rearrange("p e u c -> p e c u"),
+            )
+            codes = keep.tile([P, n * C], U32, name=f"h_codes{first}", align_bytes=64)
+            scales = keep.tile([P, n * C], U8, name=f"h_scales{first}", align_bytes=64)
+            nc.vector.quantize_mx(out=codes[:].bitcast(FP8X4), scales=scales[:], in_=grouped[:])
+            for e in range(first, last):
+                cols = slice((e - first) * C, (e - first + 1) * C)
+                hq[e] = (codes[:, cols], scales[:, cols])
+
+        def second_layer(e, m, dst):
+            nc.tensor.matmul_mx(
+                out=dst,
+                lhsT=expert_words(w2w, SECOND_CHUNKS, e)[:, 2 * P * m : 2 * P * (m + 1)].bitcast(FP4X4),
+                lhsT_scale=w2s[:, e, P * m : P * (m + 1)],
+                rhs=hq[e][0].bitcast(FP8X4),
+                rhs_scale=hq[e][1],
+                start=True,
+                stop=True,
+            )
+
+        y_bank = {}
+
+        def finish_group(first, last):
+            turn_and_quantize(first, last)
+            for e in range(first, last):
+                lo, hi = [span for span in Y_BANKS if span[0] <= e < span[1]][0]
+                if e == lo:
+                    y_bank[lo] = psum.tile([P, (hi - lo) * C], F32, name="y_bank")
+                second_layer(e, 0, y_bank[lo][:, (e - lo) * C : (e - lo + 1) * C])
+                if e == hi - 1:
+                    if hi == E:
+                        nc.vector.tensor_copy(y[0][:, lo * C : hi * C], y_bank[lo][:])
+                    else:
+                        nc.scalar.copy(y[0][:, lo * C : hi * C], y_bank[lo][:])
+
+        gather(xw[:], U32, WORD_PIECES, slot_words, "slot_words")
+        gather(xs[:, 0, :], U8, SCALE_PIECES, slot_scales, "slot_scales")
+        ends = {last: (first, last) for first, last in SECOND_GROUPS}
+        for e in range(E):
+            first_layer(e)
+            if e in ends:
+                finish_group(*ends[e])
+        finish_group(*ends[E])
+
+        for half in range(2):
+            bank = psum.tile([P, 4 * C], F32, name="a")
+            for e in range(4 * half, 4 * half + 4):
+                second_layer(e, 1, bank[:, (e % 4) * C : (e % 4 + 1) * C])
+            nc.scalar.copy(y[1][:, 4 * C * half : 4 * C * (half + 1)], bank[:])
+
+        parts = [[keep.tile([P, T], F32, name=f"part{m}{j}") for j in range(2)] for m in range(2)]
+
+        def fetch(m, j, lo, hi):
+            nc.vector.tensor_tensor(
+                parts[m][j][:, lo:hi], y[m][:].indirect(pos_sb[j][:, lo // 16 : hi // 16]), gate_sb[j][:, lo:hi], MULT
+            )
+
+        def add_and_store(m, lo, hi):
+            total = keep.tile([P, hi - lo], F32, name=f"total{m}_{lo}")
+            nc.vector.tensor_tensor(total[:], parts[m][0][:, lo:hi], parts[m][1][:, lo:hi], ADD)
+            nc.sync.dma_start(out=out[m * P : (m + 1) * P, lo:hi], in_=total[:])
+
+        fetch(0, 0, 0, T)
+        fetch(0, 1, 0, T)
+        fetch(1, 0, 0, T)
+        add_and_store(0, 0, T)
+        fetch(1, 1, 0, T // 2)
+        fetch(1, 1, T // 2, T)
+        add_and_store(1, 0, T // 2)
+        add_and_store(1, T // 2, T)

@@ -20,12 +20,13 @@ MULT = mybir.AluOpType.mult
 ADD = mybir.AluOpType.add
 
 P = 128
-WORD_PIECES = ((0, 3), (3, 6), (6, 8))
+WORD_PIECES = ((0, 2), (2, 4), (4, 6), (6, 8))
 SCALE_PIECES = ((0, 2), (2, 5), (5, 8))
-FIRST_CHUNKS = ((0, 3), (3, 5), (5, 8))
+W1_CHUNKS = ((0, 2), (2, 5), (5, 8))
+W3_CHUNKS = ((0, 2), (2, 4), (4, 6), (6, 8))
 SECOND_CHUNKS = ((0, 4), (4, 8))
 SECOND_GROUPS = ((0, 2), (2, 4), (4, 6), (6, 7), (7, 8))
-Y_BANKS = ((0, 4), (4, 7), (7, 8))
+Y_BANKS = ((0, 4), (4, 6), (6, 8))
 
 
 def load_scale_rows(queue, plane, rows):
@@ -50,17 +51,15 @@ def tile_moe_pkd_glu_sigmoid_kernel(
         w1s = keep.tile([P, E, H], U8, name="w1s", align_bytes=64)
         w3s = keep.tile([P, E, H], U8, name="w3s", align_bytes=64)
         w2s = keep.tile([P, E, N], U8, name="w2s", align_bytes=64)
-        w1w = {a: keep.tile([P, b - a, 2 * H], U8, name=f"w1w{a}", align_bytes=64) for a, b in FIRST_CHUNKS}
-        w3w = {a: keep.tile([P, b - a, 2 * H], U8, name=f"w3w{a}", align_bytes=64) for a, b in FIRST_CHUNKS}
+        w1w = {a: keep.tile([P, b - a, 2 * H], U8, name=f"w1w{a}", align_bytes=64) for a, b in W1_CHUNKS}
+        w3w = {a: keep.tile([P, b - a, 2 * H], U8, name=f"w3w{a}", align_bytes=64) for a, b in W3_CHUNKS}
         w2w = {a: keep.tile([P, b - a, 2 * N], U8, name=f"w2w{a}", align_bytes=64) for a, b in SECOND_CHUNKS}
         gate_sb = [keep.tile([P, T], F32, name=f"gate_sb{j}") for j in range(2)]
         ident = keep.tile([P, P], F32, name="ident")
         y = [keep.tile([P, S], F32, name=f"y{m}") for m in range(2)]
 
-        for plane in (w1s, xs, w3s):
-            nc.vector.memset(plane[:].bitcast(I32), 0)
-        nc.gpsimd.memset(w2s[:].bitcast(I32), 0)
-        load_scale_rows(nc.gpsimd, w2s, w2_scales[:, 0])
+        for engine, plane in ((nc.vector, xs), (nc.gpsimd, w3s), (nc.vector, w1s), (nc.vector, w2s)):
+            engine.memset(plane[:].bitcast(I32), 0)
         make_identity(nc, ident[:])
 
         def load_words(tiles, words, chunk):
@@ -73,16 +72,17 @@ def tile_moe_pkd_glu_sigmoid_kernel(
 
         nc.sync.dma_start(out=xw[:].bitcast(I32), in_=x_words[0].rearrange("p t r -> p (t r)").bitcast(I32))
         nc.sync.dma_start(offs_sb[:], offs)
-        load_scale_rows(nc.sync, w1s, w1_scales[:, 0])
-        load_words(w1w, w1_words, FIRST_CHUNKS[0])
         load_scale_rows(nc.sync, xs, x_scales)
-        load_words(w3w, w3_words, FIRST_CHUNKS[0])
+        load_words(w1w, w1_words, W1_CHUNKS[0])
+        load_words(w3w, w3_words, W3_CHUNKS[0])
+        load_scale_rows(nc.sync, w1s, w1_scales[:, 0])
         load_scale_rows(nc.sync, w3s, w3_scales[:, 0])
-        load_words(w1w, w1_words, FIRST_CHUNKS[1])
-        load_words(w3w, w3_words, FIRST_CHUNKS[1])
+        for i in (1, 2):
+            load_words(w1w, w1_words, W1_CHUNKS[i])
+            load_words(w3w, w3_words, W3_CHUNKS[i])
+        load_words(w3w, w3_words, W3_CHUNKS[3])
         load_words(w2w, w2_words, SECOND_CHUNKS[0])
-        load_words(w1w, w1_words, FIRST_CHUNKS[2])
-        load_words(w3w, w3_words, FIRST_CHUNKS[2])
+        load_scale_rows(nc.sync, w2s, w2_scales[:, 0])
         load_words(w2w, w2_words, SECOND_CHUNKS[1])
         nc.sync.dma_start(pos_sb[0][:], pos1)
         nc.sync.dma_start(pos_sb[1][:], pos2)
@@ -97,7 +97,7 @@ def tile_moe_pkd_glu_sigmoid_kernel(
         def gather(window, dtype, pieces, found, label):
             for first, last in pieces:
                 entries = offs_sb[:, first * C // 16 : last * C // 16]
-                got = keep.tile([P, (last - first) * C], dtype, name=f"{label}{first}", align_bytes=64)
+                got = ring.tile([P, (last - first) * C], dtype, name=label, bufs=3, align_bytes=64)
                 nc.vector.tensor_copy(got[:], window.indirect(entries))
                 for e in range(first, last):
                     found[e] = got[:, (e - first) * C : (e - first + 1) * C]
@@ -105,12 +105,12 @@ def tile_moe_pkd_glu_sigmoid_kernel(
         def first_layer(e):
             a = psum.tile([P, H], F32, name="a")
             b = psum.tile([P, H], F32, name="b")
-            for acc, words, scales in ((a, w1w, w1s), (b, w3w, w3s)):
+            for acc, words, chunks, scales in ((a, w1w, W1_CHUNKS, w1s), (b, w3w, W3_CHUNKS, w3s)):
                 nc.tensor.matmul_mx(
                     out=acc[:],
                     lhsT=slot_words[e].bitcast(FP8X4),
                     lhsT_scale=slot_scales[e],
-                    rhs=expert_words(words, FIRST_CHUNKS, e).bitcast(FP4X4),
+                    rhs=expert_words(words, chunks, e).bitcast(FP4X4),
                     rhs_scale=scales[:, e, :],
                     start=True,
                     stop=True,
@@ -166,19 +166,21 @@ def tile_moe_pkd_glu_sigmoid_kernel(
             for e in range(first, last):
                 lo, hi = [span for span in Y_BANKS if span[0] <= e < span[1]][0]
                 if e == lo:
-                    y_bank[lo] = psum.tile([P, (hi - lo) * C], F32, name="y_bank")
+                    y_bank[lo] = psum.tile([P, (hi - lo) * C], F32, name="a" if hi == E else "y_bank")
                 second_layer(e, 0, y_bank[lo][:, (e - lo) * C : (e - lo + 1) * C])
                 if e == hi - 1:
-                    if hi == E:
+                    if lo > 0:
                         nc.vector.tensor_copy(y[0][:, lo * C : hi * C], y_bank[lo][:])
                     else:
                         nc.scalar.copy(y[0][:, lo * C : hi * C], y_bank[lo][:])
 
-        gather(xw[:], U32, WORD_PIECES, slot_words, "slot_words")
+        gather(xw[:], U32, WORD_PIECES[:-1], slot_words, "slot_words")
         gather(xs[:, 0, :], U8, SCALE_PIECES, slot_scales, "slot_scales")
         ends = {last: (first, last) for first, last in SECOND_GROUPS}
         for e in range(E):
             first_layer(e)
+            if e == 1:
+                gather(xw[:], U32, WORD_PIECES[-1:], slot_words, "slot_words")
             if e in ends:
                 finish_group(*ends[e])
         finish_group(*ends[E])

@@ -26,7 +26,6 @@ W1_CHUNKS = ((0, 2), (2, 5), (5, 8))
 W3_CHUNKS = ((0, 2), (2, 4), (4, 6), (6, 8))
 SECOND_CHUNKS = ((0, 4), (4, 8))
 SECOND_GROUPS = ((0, 2), (2, 4), (4, 6), (6, 7), (7, 8))
-Y_BANKS = ((0, 4), (4, 6), (6, 8))
 
 
 def load_scale_rows(queue, plane, rows):
@@ -92,7 +91,7 @@ def tile_moe_pkd_glu_sigmoid_kernel(
         slot_words = {}
         slot_scales = {}
         h = {}
-        hq = {}
+        grouped = {}
 
         def gather(window, dtype, pieces, found, label):
             for first, last in pieces:
@@ -103,8 +102,8 @@ def tile_moe_pkd_glu_sigmoid_kernel(
                     found[e] = got[:, (e - first) * C : (e - first + 1) * C]
 
         def first_layer(e):
-            a = psum.tile([P, H], F32, name="a")
-            b = psum.tile([P, H], F32, name="b")
+            a = psum.tile([P, H], F32, name="a", bufs=3)
+            b = psum.tile([P, H], F32, name="b", bufs=3)
             for acc, words, chunks, scales in ((a, w1w, W1_CHUNKS, w1s), (b, w3w, W3_CHUNKS, w3s)):
                 nc.tensor.matmul_mx(
                     out=acc[:],
@@ -115,81 +114,83 @@ def tile_moe_pkd_glu_sigmoid_kernel(
                     start=True,
                     stop=True,
                 )
-            sig = ring.tile([P, H], F32, name="sig", bufs=E)
-            h[e] = ring.tile([P, H], BF16, name="h", bufs=4)
+            if e == E - 1:
+                sig = keep.tile([P, H], F32, name="last_sig_then_codes", align_bytes=64)
+            else:
+                sig = ring.tile([P, H], F32, name="sig", bufs=E - 1)
+            if e == 2:
+                middle_h = keep.tile([P, 4, H], BF16, name="middle_h")
+                for j in range(4):
+                    h[2 + j] = middle_h[:, j, :]
+            if e not in h:
+                h[e] = keep.tile([P, H], BF16, name=f"h{e}")[:]
             nc.scalar.activation(
                 out=sig[:].rearrange("c (u p d) -> c u p d", u=2, d=2),
                 in_=a[:].rearrange("c (p u d) -> c u p d", u=2, d=2),
                 func=SIGMOID,
             )
             nc.vector.tensor_tensor(
-                out=h[e][:].rearrange("c (u p d) -> c u p d", u=2, d=2),
+                out=h[e].rearrange("c (u p d) -> c u p d", u=2, d=2),
                 in0=b[:].rearrange("c (p u d) -> c u p d", u=2, d=2),
                 in1=sig[:].rearrange("c (u p d) -> c u p d", u=2, d=2),
                 op=MULT,
             )
 
-        def turn_and_quantize(first, last):
+        def turn(first, last):
             n = last - first
-            turned = psum.tile([P, n, 2, C], F32, name="turned")
+            if n == 1:
+                turned = psum.tile([P, n, 2, C], F32, name="b", bufs=3)
+            else:
+                turned = psum.tile([P, n, 2, C], F32, name="turned")
             for e in range(first, last):
-                pairs = h[e][:].bitcast(F32)
+                pairs = h[e].bitcast(F32)
                 for u in range(2):
                     nc.tensor.transpose(turned[:, e - first, u, :], pairs[:, u * P : (u + 1) * P], ident[:])
-            grouped = ring.tile([P, n * C * 4], BF16, name="grouped", align_bytes=64)
+            grouped[first] = keep.tile([P, n * C * 4], BF16, name=f"grouped{first}", align_bytes=64)
             nc.scalar.copy(
-                out=grouped[:].bitcast(F32).rearrange("p (e c u) -> p e c u", e=n, u=2),
+                out=grouped[first][:].bitcast(F32).rearrange("p (e c u) -> p e c u", e=n, u=2),
                 in_=turned[:].rearrange("p e u c -> p e c u"),
             )
-            codes = keep.tile([P, n * C], U32, name=f"h_codes{first}", align_bytes=64)
-            scales = keep.tile([P, n * C], U8, name=f"h_scales{first}", align_bytes=64)
-            nc.vector.quantize_mx(out=codes[:].bitcast(FP8X4), scales=scales[:], in_=grouped[:])
-            for e in range(first, last):
-                cols = slice((e - first) * C, (e - first + 1) * C)
-                hq[e] = (codes[:, cols], scales[:, cols])
 
         def second_layer(e, m, dst):
             nc.tensor.matmul_mx(
                 out=dst,
                 lhsT=expert_words(w2w, SECOND_CHUNKS, e)[:, 2 * P * m : 2 * P * (m + 1)].bitcast(FP4X4),
                 lhsT_scale=w2s[:, e, P * m : P * (m + 1)],
-                rhs=hq[e][0].bitcast(FP8X4),
-                rhs_scale=hq[e][1],
+                rhs=h_codes[:, e * C : (e + 1) * C].bitcast(FP8X4),
+                rhs_scale=h_scales[:, e * C : (e + 1) * C],
                 start=True,
                 stop=True,
             )
 
-        y_bank = {}
-
-        def finish_group(first, last):
-            turn_and_quantize(first, last)
+        def second_layer_bank(first, last, m, copy):
+            bank = psum.tile([P, (last - first) * C], F32, name="a", bufs=3)
             for e in range(first, last):
-                lo, hi = [span for span in Y_BANKS if span[0] <= e < span[1]][0]
-                if e == lo:
-                    y_bank[lo] = psum.tile([P, (hi - lo) * C], F32, name="a" if hi == E else "y_bank")
-                second_layer(e, 0, y_bank[lo][:, (e - lo) * C : (e - lo + 1) * C])
-                if e == hi - 1:
-                    if lo > 0:
-                        nc.vector.tensor_copy(y[0][:, lo * C : hi * C], y_bank[lo][:])
-                    else:
-                        nc.scalar.copy(y[0][:, lo * C : hi * C], y_bank[lo][:])
+                second_layer(e, m, bank[:, (e - first) * C : (e - first + 1) * C])
+            copy(y[m][:, first * C : last * C], bank[:])
 
         gather(xw[:], U32, WORD_PIECES[:-1], slot_words, "slot_words")
         gather(xs[:, 0, :], U8, SCALE_PIECES, slot_scales, "slot_scales")
-        ends = {last: (first, last) for first, last in SECOND_GROUPS}
         for e in range(E):
             first_layer(e)
             if e == 1:
                 gather(xw[:], U32, WORD_PIECES[-1:], slot_words, "slot_words")
-            if e in ends:
-                finish_group(*ends[e])
-        finish_group(*ends[E])
+            if e == 3:
+                turn(*SECOND_GROUPS[0])
+        for group in SECOND_GROUPS[1:]:
+            turn(*group)
 
-        for half in range(2):
-            bank = psum.tile([P, 4 * C], F32, name="a")
-            for e in range(4 * half, 4 * half + 4):
-                second_layer(e, 1, bank[:, (e % 4) * C : (e % 4 + 1) * C])
-            nc.scalar.copy(y[1][:, 4 * C * half : 4 * C * (half + 1)], bank[:])
+        h_codes = keep.tile([P, S], U32, name="last_sig_then_codes", align_bytes=64)
+        h_scales = keep.tile([P, S], U8, name="h_scales", align_bytes=64)
+        for first, last in SECOND_GROUPS:
+            cols = slice(first * C, last * C)
+            nc.vector.quantize_mx(out=h_codes[:, cols].bitcast(FP8X4), scales=h_scales[:, cols], in_=grouped[first][:])
+
+        second_layer_bank(0, 4, 0, nc.scalar.copy)
+        second_layer_bank(4, 6, 0, nc.scalar.copy)
+        second_layer_bank(6, 8, 0, nc.vector.tensor_copy)
+        second_layer_bank(0, 4, 1, nc.scalar.copy)
+        second_layer_bank(4, 8, 1, nc.scalar.copy)
 
         parts = [[keep.tile([P, T], F32, name=f"part{m}{j}") for j in range(2)] for m in range(2)]
 

@@ -16,22 +16,39 @@ U8 = mybir.dt.uint8
 FP8X4 = mybir.dt.float8_e4m3fn_x4
 FP4X4 = mybir.dt.float4_e2m1fn_x4
 SIGMOID = mybir.ActivationFunctionType.Sigmoid
+COPY = mybir.ActivationFunctionType.Copy
 MULT = mybir.AluOpType.mult
 ADD = mybir.AluOpType.add
 
 P = 128
+PER_COLUMN = 16
+HALF = T // 2
+
 WORD_PIECES = ((0, 2), (2, 4), (4, 6), (6, 8))
 SCALE_PIECES = ((0, 2), (2, 5), (5, 8))
+GATHER_DEPTH = 3
 W1_CHUNKS = ((0, 2), (2, 5), (5, 8))
 W3_CHUNKS = ((0, 2), (2, 4), (4, 6), (6, 8))
-SECOND_CHUNKS = ((0, 4), (4, 8))
-SECOND_GROUPS = ((0, 2), (2, 4), (4, 6), (6, 7), (7, 8))
+W2_CHUNKS = ((0, 4), (4, 8))
+TURN_GROUPS = ((0, 2), (2, 4), (4, 6), (6, 7), (7, 8))
+MIDDLE = (2, 6)
+BANKS = {"a": 3, "b": 3, "turned": 2}
 
 
-def load_scale_rows(queue, plane, rows):
+def load_scale_rows(nc, plane, rows):
     by_r = rows.rearrange("e (q r) n -> r q e n", r=4)
     for r in range(4):
-        queue.dma_start(out=plane[r:P:32].bitcast(I32), in_=by_r[r].bitcast(I32))
+        nc.sync.dma_start(out=plane[r:P:32].bitcast(I32), in_=by_r[r].bitcast(I32))
+
+
+def load_words(nc, tiles, words, chunk):
+    src = words[chunk[0] : chunk[1], 0].rearrange("e p b -> p e b")
+    nc.sync.dma_start(out=tiles[chunk[0]][:].bitcast(I32), in_=src.bitcast(I32))
+
+
+def expert_words(tiles, chunks, e):
+    first = [lo for lo, hi in chunks if lo <= e < hi][0]
+    return tiles[first][:, e - first, :]
 
 
 def tile_moe_pkd_glu_sigmoid_kernel(
@@ -40,20 +57,24 @@ def tile_moe_pkd_glu_sigmoid_kernel(
     nc = tc.nc
     with ExitStack() as ctx:
         keep = ctx.enter_context(tc.tile_pool(name="keep", bufs=1))
-        ring = ctx.enter_context(tc.tile_pool(name="ring", bufs=2))
-        psum = ctx.enter_context(tc.psum_pool(name="psum", bufs=2))
+        ring = ctx.enter_context(tc.tile_pool(name="ring", bufs=GATHER_DEPTH))
+        psum = ctx.enter_context(tc.psum_pool(name="psum", bufs=1))
 
-        offs_sb = keep.tile([P, S // 16], U16, name="offs_sb")
-        pos_sb = [keep.tile([P, T // 16], U16, name=f"pos_sb{j}") for j in range(2)]
+        def bank(tag, shape):
+            return psum.tile(shape, F32, name=tag, bufs=BANKS[tag])
+
+        offs_sb = keep.tile([P, S // PER_COLUMN], U16, name="offs_sb")
+        pos_sb = [keep.tile([P, T // PER_COLUMN], U16, name=f"pos_sb{j}") for j in range(2)]
         xw = keep.tile([P, T], U32, name="xw", align_bytes=64)
         xs = keep.tile([P, 1, T], U8, name="xs", align_bytes=64)
         w1s = keep.tile([P, E, H], U8, name="w1s", align_bytes=64)
         w3s = keep.tile([P, E, H], U8, name="w3s", align_bytes=64)
         w2s = keep.tile([P, E, N], U8, name="w2s", align_bytes=64)
-        w1w = {a: keep.tile([P, b - a, 2 * H], U8, name=f"w1w{a}", align_bytes=64) for a, b in W1_CHUNKS}
-        w3w = {a: keep.tile([P, b - a, 2 * H], U8, name=f"w3w{a}", align_bytes=64) for a, b in W3_CHUNKS}
-        w2w = {a: keep.tile([P, b - a, 2 * N], U8, name=f"w2w{a}", align_bytes=64) for a, b in SECOND_CHUNKS}
-        gate_sb = [keep.tile([P, T], F32, name=f"gate_sb{j}") for j in range(2)]
+        w1w = {lo: keep.tile([P, hi - lo, 2 * H], U8, name=f"w1w{lo}", align_bytes=64) for lo, hi in W1_CHUNKS}
+        w3w = {lo: keep.tile([P, hi - lo, 2 * H], U8, name=f"w3w{lo}", align_bytes=64) for lo, hi in W3_CHUNKS}
+        w2w = {lo: keep.tile([P, hi - lo, 2 * N], U8, name=f"w2w{lo}", align_bytes=64) for lo, hi in W2_CHUNKS}
+        gate_rows = [keep.tile([P, T], F32, name=f"gate_rows{j}") for j in range(2)]
+        gate_cols = [keep.tile([P, T // P], F32, name=f"gate_cols{j}") for j in range(2)]
         ident = keep.tile([P, P], F32, name="ident")
         y = [keep.tile([P, S], F32, name=f"y{m}") for m in range(2)]
 
@@ -61,56 +82,51 @@ def tile_moe_pkd_glu_sigmoid_kernel(
             engine.memset(plane[:].bitcast(I32), 0)
         make_identity(nc, ident[:])
 
-        def load_words(tiles, words, chunk):
-            src = words[chunk[0] : chunk[1], 0].rearrange("e p b -> p e b")
-            nc.sync.dma_start(out=tiles[chunk[0]][:].bitcast(I32), in_=src.bitcast(I32))
-
-        def expert_words(tiles, chunks, e):
-            first = [a for a, b in chunks if a <= e < b][0]
-            return tiles[first][:, e - first, :]
-
         nc.sync.dma_start(out=xw[:].bitcast(I32), in_=x_words[0].rearrange("p t r -> p (t r)").bitcast(I32))
         nc.sync.dma_start(offs_sb[:], offs)
-        load_scale_rows(nc.sync, xs, x_scales)
-        load_words(w1w, w1_words, W1_CHUNKS[0])
-        load_words(w3w, w3_words, W3_CHUNKS[0])
-        load_scale_rows(nc.sync, w1s, w1_scales[:, 0])
-        load_scale_rows(nc.sync, w3s, w3_scales[:, 0])
-        for i in (1, 2):
-            load_words(w1w, w1_words, W1_CHUNKS[i])
-            load_words(w3w, w3_words, W3_CHUNKS[i])
-        load_words(w3w, w3_words, W3_CHUNKS[3])
-        load_words(w2w, w2_words, SECOND_CHUNKS[0])
-        load_scale_rows(nc.sync, w2s, w2_scales[:, 0])
-        load_words(w2w, w2_words, SECOND_CHUNKS[1])
+        load_scale_rows(nc, xs, x_scales)
+        load_words(nc, w1w, w1_words, W1_CHUNKS[0])
+        load_words(nc, w3w, w3_words, W3_CHUNKS[0])
+        load_scale_rows(nc, w1s, w1_scales[:, 0])
+        load_scale_rows(nc, w3s, w3_scales[:, 0])
+        for chunk in W1_CHUNKS[1:]:
+            load_words(nc, w1w, w1_words, chunk)
+            load_words(nc, w3w, w3_words, W3_CHUNKS[W1_CHUNKS.index(chunk)])
+        load_words(nc, w3w, w3_words, W3_CHUNKS[-1])
+        load_words(nc, w2w, w2_words, W2_CHUNKS[0])
+        load_scale_rows(nc, w2s, w2_scales[:, 0])
+        load_words(nc, w2w, w2_words, W2_CHUNKS[1])
         nc.sync.dma_start(pos_sb[0][:], pos1)
         nc.sync.dma_start(pos_sb[1][:], pos2)
         for j in range(2):
-            nc.sync.dma_start(out=gate_sb[j][:], in_=gate[j, 0:P, :])
+            nc.sync.dma_start(out=gate_rows[j][:], in_=gate[j, 0:P, :])
+        with nc.allow_non_contiguous_dma(reason="one gate value a token and partition"):
+            for j in range(2):
+                nc.sync.dma_start(out=gate_cols[j][:], in_=gate[j, 0, :].rearrange("(b p) -> p b", p=P))
 
         slot_words = {}
         slot_scales = {}
         h = {}
         grouped = {}
 
-        def gather(window, dtype, pieces, found, label):
+        def gather(window, dtype, pieces, found, tag):
             for first, last in pieces:
-                entries = offs_sb[:, first * C // 16 : last * C // 16]
-                got = ring.tile([P, (last - first) * C], dtype, name=label, bufs=3, align_bytes=64)
+                entries = offs_sb[:, first * C // PER_COLUMN : last * C // PER_COLUMN]
+                got = ring.tile([P, (last - first) * C], dtype, name=tag, align_bytes=64)
                 nc.vector.tensor_copy(got[:], window.indirect(entries))
                 for e in range(first, last):
                     found[e] = got[:, (e - first) * C : (e - first + 1) * C]
 
         def first_layer(e):
-            a = psum.tile([P, H], F32, name="a", bufs=3)
-            b = psum.tile([P, H], F32, name="b", bufs=3)
-            for acc, words, chunks, scales in ((a, w1w, W1_CHUNKS, w1s), (b, w3w, W3_CHUNKS, w3s)):
+            a = bank("a", [P, H])
+            b = bank("b", [P, H])
+            for acc, words, chunks, plane in ((a, w1w, W1_CHUNKS, w1s), (b, w3w, W3_CHUNKS, w3s)):
                 nc.tensor.matmul_mx(
                     out=acc[:],
                     lhsT=slot_words[e].bitcast(FP8X4),
                     lhsT_scale=slot_scales[e],
                     rhs=expert_words(words, chunks, e).bitcast(FP4X4),
-                    rhs_scale=scales[:, e, :],
+                    rhs_scale=plane[:, e, :],
                     start=True,
                     stop=True,
                 )
@@ -118,10 +134,10 @@ def tile_moe_pkd_glu_sigmoid_kernel(
                 sig = keep.tile([P, H], F32, name="last_sig_then_codes", align_bytes=64)
             else:
                 sig = ring.tile([P, H], F32, name="sig", bufs=E - 1)
-            if e == 2:
-                middle_h = keep.tile([P, 4, H], BF16, name="middle_h")
-                for j in range(4):
-                    h[2 + j] = middle_h[:, j, :]
+            if e == MIDDLE[0]:
+                middle_h = keep.tile([P, MIDDLE[1] - MIDDLE[0], H], BF16, name="middle_h")
+                for other in range(*MIDDLE):
+                    h[other] = middle_h[:, other - MIDDLE[0], :]
             if e not in h:
                 h[e] = keep.tile([P, H], BF16, name=f"h{e}")[:]
             nc.scalar.activation(
@@ -137,78 +153,97 @@ def tile_moe_pkd_glu_sigmoid_kernel(
             )
 
         def turn(first, last):
-            n = last - first
-            if n == 1:
-                turned = psum.tile([P, n, 2, C], F32, name="b", bufs=3)
-            else:
-                turned = psum.tile([P, n, 2, C], F32, name="turned")
+            count = last - first
+            turned = bank("b" if count == 1 else "turned", [P, count, 2, C])
             for e in range(first, last):
                 pairs = h[e].bitcast(F32)
                 for u in range(2):
                     nc.tensor.transpose(turned[:, e - first, u, :], pairs[:, u * P : (u + 1) * P], ident[:])
-            grouped[first] = keep.tile([P, n * C * 4], BF16, name=f"grouped{first}", align_bytes=64)
-            nc.scalar.copy(
-                out=grouped[first][:].bitcast(F32).rearrange("p (e c u) -> p e c u", e=n, u=2),
+            grouped[first] = keep.tile([P, count * C * 4], BF16, name=f"grouped{first}", align_bytes=64)
+            copy = nc.vector.tensor_copy if first == E - 2 else nc.scalar.copy
+            copy(
+                out=grouped[first][:].bitcast(F32).rearrange("p (e c u) -> p e c u", e=count, u=2),
                 in_=turned[:].rearrange("p e u c -> p e c u"),
             )
 
-        def second_layer(e, m, dst):
-            nc.tensor.matmul_mx(
-                out=dst,
-                lhsT=expert_words(w2w, SECOND_CHUNKS, e)[:, 2 * P * m : 2 * P * (m + 1)].bitcast(FP4X4),
-                lhsT_scale=w2s[:, e, P * m : P * (m + 1)],
-                rhs=h_codes[:, e * C : (e + 1) * C].bitcast(FP8X4),
-                rhs_scale=h_scales[:, e * C : (e + 1) * C],
-                start=True,
-                stop=True,
-            )
-
-        def second_layer_bank(first, last, m, copy):
-            bank = psum.tile([P, (last - first) * C], F32, name="a", bufs=3)
-            for e in range(first, last):
-                second_layer(e, m, bank[:, (e - first) * C : (e - first + 1) * C])
-            copy(y[m][:, first * C : last * C], bank[:])
-
-        gather(xw[:], U32, WORD_PIECES[:-1], slot_words, "slot_words")
+        gather(xw[:], U32, WORD_PIECES[:GATHER_DEPTH], slot_words, "slot_words")
         gather(xs[:, 0, :], U8, SCALE_PIECES, slot_scales, "slot_scales")
         for e in range(E):
             first_layer(e)
-            if e == 1:
-                gather(xw[:], U32, WORD_PIECES[-1:], slot_words, "slot_words")
-            if e == 3:
-                turn(*SECOND_GROUPS[0])
-        for group in SECOND_GROUPS[1:]:
+            if e == WORD_PIECES[0][1] - 1:
+                gather(xw[:], U32, WORD_PIECES[GATHER_DEPTH:], slot_words, "slot_words")
+            if e == TURN_GROUPS[1][1] - 1:
+                turn(*TURN_GROUPS[0])
+        for group in TURN_GROUPS[1:]:
             turn(*group)
 
         h_codes = keep.tile([P, S], U32, name="last_sig_then_codes", align_bytes=64)
         h_scales = keep.tile([P, S], U8, name="h_scales", align_bytes=64)
-        for first, last in SECOND_GROUPS:
-            cols = slice(first * C, last * C)
-            nc.vector.quantize_mx(out=h_codes[:, cols].bitcast(FP8X4), scales=h_scales[:, cols], in_=grouped[first][:])
+        for first, last in TURN_GROUPS:
+            slots = slice(first * C, last * C)
+            nc.vector.quantize_mx(out=h_codes[:, slots].bitcast(FP8X4), scales=h_scales[:, slots], in_=grouped[first][:])
 
-        second_layer_bank(0, 4, 0, nc.scalar.copy)
-        second_layer_bank(4, 6, 0, nc.scalar.copy)
-        second_layer_bank(6, 8, 0, nc.vector.tensor_copy)
-        second_layer_bank(0, 4, 1, nc.scalar.copy)
-        second_layer_bank(4, 8, 1, nc.scalar.copy)
+        def second_layer(first, last, m, copy):
+            acc = bank("a", [P, (last - first) * C])
+            for e in range(first, last):
+                slots = slice(e * C, (e + 1) * C)
+                nc.tensor.matmul_mx(
+                    out=acc[:, (e - first) * C : (e - first + 1) * C],
+                    lhsT=expert_words(w2w, W2_CHUNKS, e)[:, 2 * P * m : 2 * P * (m + 1)].bitcast(FP4X4),
+                    lhsT_scale=w2s[:, e, P * m : P * (m + 1)],
+                    rhs=h_codes[:, slots].bitcast(FP8X4),
+                    rhs_scale=h_scales[:, slots],
+                    start=True,
+                    stop=True,
+                )
+            copy(y[m][:, first * C : last * C], acc[:])
 
-        parts = [[keep.tile([P, T], F32, name=f"part{m}{j}") for j in range(2)] for m in range(2)]
+        second_layer(0, 4, 0, nc.scalar.copy)
+        second_layer(4, 6, 0, nc.scalar.copy)
+        second_layer(6, 8, 0, nc.vector.tensor_copy)
+        second_layer(0, 4, 1, nc.scalar.copy)
+        second_layer(4, 8, 1, nc.scalar.copy)
 
-        def fetch(m, j, lo, hi):
+        for lo in (0, HALF):
+            entries = slice(lo // PER_COLUMN, (lo + HALF) // PER_COLUMN)
+            blocks = range(HALF // P)
+            gated = []
+            for j in range(2):
+                fetched = keep.tile([P, HALF], F32, name=f"fetched{j}_{lo}")
+                nc.vector.tensor_copy(fetched[:], y[0][:].indirect(pos_sb[j][:, entries]))
+                by_token = bank("turned" if lo == 0 else "a", [P, HALF])
+                for blk in blocks:
+                    cols = slice(blk * P, (blk + 1) * P)
+                    nc.tensor.transpose(by_token[:, cols], fetched[:, cols], ident[:])
+                gated.append(keep.tile([P, HALF], F32, name=f"gated{j}_{lo}"))
+                for blk in blocks:
+                    cols = slice(blk * P, (blk + 1) * P)
+                    token_block = lo // P + blk
+                    scale = gate_cols[j][:, token_block : token_block + 1]
+                    nc.scalar.activation(out=gated[j][:, cols], in_=by_token[:, cols], func=COPY, scale=scale)
+            summed = bank("b", [P, HALF])
+            for blk in blocks:
+                cols = slice(blk * P, (blk + 1) * P)
+                for j in range(2):
+                    nc.tensor.matmul(
+                        summed[:, cols],
+                        lhsT=gated[j][:, cols],
+                        rhs=ident[:],
+                        start=(j == 0),
+                        stop=(j == 1),
+                        is_transpose=True,
+                    )
+            total = keep.tile([P, HALF], F32, name=f"total0_{lo}")
+            nc.scalar.copy(total[:], summed[:])
+            nc.sync.dma_start(out=out[0:P, lo : lo + HALF], in_=total[:])
+
+        parts = [keep.tile([P, T], F32, name=f"part{j}") for j in range(2)]
+        for j, lo, hi in ((0, 0, T), (1, 0, HALF), (1, HALF, T)):
+            entries = slice(lo // PER_COLUMN, hi // PER_COLUMN)
             nc.vector.tensor_tensor(
-                parts[m][j][:, lo:hi], y[m][:].indirect(pos_sb[j][:, lo // 16 : hi // 16]), gate_sb[j][:, lo:hi], MULT
+                parts[j][:, lo:hi], y[1][:].indirect(pos_sb[j][:, entries]), gate_rows[j][:, lo:hi], MULT
             )
-
-        def add_and_store(m, lo, hi):
-            total = keep.tile([P, hi - lo], F32, name=f"total{m}_{lo}")
-            nc.vector.tensor_tensor(total[:], parts[m][0][:, lo:hi], parts[m][1][:, lo:hi], ADD)
-            nc.sync.dma_start(out=out[m * P : (m + 1) * P, lo:hi], in_=total[:])
-
-        fetch(0, 0, 0, T)
-        fetch(0, 1, 0, T)
-        fetch(1, 0, 0, T)
-        add_and_store(0, 0, T)
-        fetch(1, 1, 0, T // 2)
-        fetch(1, 1, T // 2, T)
-        add_and_store(1, 0, T // 2)
-        add_and_store(1, T // 2, T)
+        for lo in (0, HALF):
+            total = keep.tile([P, HALF], F32, name=f"total1_{lo}")
+            nc.vector.tensor_tensor(total[:], parts[0][:, lo : lo + HALF], parts[1][:, lo : lo + HALF], ADD)
+            nc.sync.dma_start(out=out[P : 2 * P, lo : lo + HALF], in_=total[:])

from contextlib import ExitStack

import concourse.mybir as mybir
from concourse.masks import make_identity

K, T, E, C, H, N = 512, 512, 8, 128, 512, 256
S = E * C
FLOPS = 2 * S * (2 * K * H + H * N)

F32 = mybir.dt.float32
BF16 = mybir.dt.bfloat16
I32 = mybir.dt.int32
U32 = mybir.dt.uint32
U16 = mybir.dt.uint16
U8 = mybir.dt.uint8
FP8X4 = mybir.dt.float8_e4m3fn_x4
FP4X4 = mybir.dt.float4_e2m1fn_x4
SIGMOID = mybir.ActivationFunctionType.Sigmoid
COPY = mybir.ActivationFunctionType.Copy
MULT = mybir.AluOpType.mult
ADD = mybir.AluOpType.add

P = 128
PER_COLUMN = 16
HALF = T // 2

WORD_PIECES = ((0, 2), (2, 4), (4, 6), (6, 8))
SCALE_PIECES = ((0, 2), (2, 5), (5, 8))
GATHER_DEPTH = 3
W1_CHUNKS = ((0, 2), (2, 5), (5, 8))
W3_CHUNKS = ((0, 2), (2, 4), (4, 6), (6, 8))
W2_CHUNKS = ((0, 4), (4, 8))
TURN_GROUPS = ((0, 2), (2, 4), (4, 6), (6, 7), (7, 8))
MIDDLE = (2, 6)
BANKS = {"a": 3, "b": 3, "turned": 2}


def load_scale_rows(nc, plane, rows):
    by_r = rows.rearrange("e (q r) n -> r q e n", r=4)
    for r in range(4):
        nc.sync.dma_start(out=plane[r:P:32].bitcast(I32), in_=by_r[r].bitcast(I32))


def load_words(nc, tiles, words, chunk):
    src = words[chunk[0] : chunk[1], 0].rearrange("e p b -> p e b")
    nc.sync.dma_start(out=tiles[chunk[0]][:].bitcast(I32), in_=src.bitcast(I32))


def expert_words(tiles, chunks, e):
    first = [lo for lo, hi in chunks if lo <= e < hi][0]
    return tiles[first][:, e - first, :]


def tile_moe_pkd_glu_sigmoid_kernel(
    tc, x_words, x_scales, w1_words, w1_scales, w3_words, w3_scales, w2_words, w2_scales, gate, offs, pos1, pos2, out
):
    nc = tc.nc
    with ExitStack() as ctx:
        keep = ctx.enter_context(tc.tile_pool(name="keep", bufs=1))
        ring = ctx.enter_context(tc.tile_pool(name="ring", bufs=GATHER_DEPTH))
        psum = ctx.enter_context(tc.psum_pool(name="psum", bufs=1))

        def bank(tag, shape):
            return psum.tile(shape, F32, name=tag, bufs=BANKS[tag])

        offs_sb = keep.tile([P, S // PER_COLUMN], U16, name="offs_sb")
        pos_sb = [keep.tile([P, T // PER_COLUMN], U16, name=f"pos_sb{j}") for j in range(2)]
        xw = keep.tile([P, T], U32, name="xw", align_bytes=64)
        xs = keep.tile([P, 1, T], U8, name="xs", align_bytes=64)
        w1s = keep.tile([P, E, H], U8, name="w1s", align_bytes=64)
        w3s = keep.tile([P, E, H], U8, name="w3s", align_bytes=64)
        w2s = keep.tile([P, E, N], U8, name="w2s", align_bytes=64)
        w1w = {lo: keep.tile([P, hi - lo, 2 * H], U8, name=f"w1w{lo}", align_bytes=64) for lo, hi in W1_CHUNKS}
        w3w = {lo: keep.tile([P, hi - lo, 2 * H], U8, name=f"w3w{lo}", align_bytes=64) for lo, hi in W3_CHUNKS}
        w2w = {lo: keep.tile([P, hi - lo, 2 * N], U8, name=f"w2w{lo}", align_bytes=64) for lo, hi in W2_CHUNKS}
        gate_rows = [keep.tile([P, T], F32, name=f"gate_rows{j}") for j in range(2)]
        gate_cols = [keep.tile([P, T // P], F32, name=f"gate_cols{j}") for j in range(2)]
        ident = keep.tile([P, P], F32, name="ident")
        y = [keep.tile([P, S], F32, name=f"y{m}") for m in range(2)]

        for engine, plane in ((nc.vector, xs), (nc.gpsimd, w3s), (nc.vector, w1s), (nc.vector, w2s)):
            engine.memset(plane[:].bitcast(I32), 0)
        make_identity(nc, ident[:])

        nc.sync.dma_start(out=xw[:].bitcast(I32), in_=x_words[0].rearrange("p t r -> p (t r)").bitcast(I32))
        nc.sync.dma_start(offs_sb[:], offs)
        load_scale_rows(nc, xs, x_scales)
        load_words(nc, w1w, w1_words, W1_CHUNKS[0])
        load_words(nc, w3w, w3_words, W3_CHUNKS[0])
        load_scale_rows(nc, w1s, w1_scales[:, 0])
        load_scale_rows(nc, w3s, w3_scales[:, 0])
        for chunk in W1_CHUNKS[1:]:
            load_words(nc, w1w, w1_words, chunk)
            load_words(nc, w3w, w3_words, W3_CHUNKS[W1_CHUNKS.index(chunk)])
        load_words(nc, w3w, w3_words, W3_CHUNKS[-1])
        load_words(nc, w2w, w2_words, W2_CHUNKS[0])
        load_scale_rows(nc, w2s, w2_scales[:, 0])
        load_words(nc, w2w, w2_words, W2_CHUNKS[1])
        nc.sync.dma_start(pos_sb[0][:], pos1)
        nc.sync.dma_start(pos_sb[1][:], pos2)
        for j in range(2):
            nc.sync.dma_start(out=gate_rows[j][:], in_=gate[j, 0:P, :])
        with nc.allow_non_contiguous_dma(reason="one gate value a token and partition"):
            for j in range(2):
                nc.sync.dma_start(out=gate_cols[j][:], in_=gate[j, 0, :].rearrange("(b p) -> p b", p=P))

        slot_words = {}
        slot_scales = {}
        h = {}
        grouped = {}

        def gather(window, dtype, pieces, found, tag):
            for first, last in pieces:
                entries = offs_sb[:, first * C // PER_COLUMN : last * C // PER_COLUMN]
                got = ring.tile([P, (last - first) * C], dtype, name=tag, align_bytes=64)
                nc.vector.tensor_copy(got[:], window.indirect(entries))
                for e in range(first, last):
                    found[e] = got[:, (e - first) * C : (e - first + 1) * C]

        def first_layer(e):
            a = bank("a", [P, H])
            b = bank("b", [P, H])
            for acc, words, chunks, plane in ((a, w1w, W1_CHUNKS, w1s), (b, w3w, W3_CHUNKS, w3s)):
                nc.tensor.matmul_mx(
                    out=acc[:],
                    lhsT=slot_words[e].bitcast(FP8X4),
                    lhsT_scale=slot_scales[e],
                    rhs=expert_words(words, chunks, e).bitcast(FP4X4),
                    rhs_scale=plane[:, e, :],
                    start=True,
                    stop=True,
                )
            if e == E - 1:
                sig = keep.tile([P, H], F32, name="last_sig_then_codes", align_bytes=64)
            else:
                sig = ring.tile([P, H], F32, name="sig", bufs=E - 1)
            if e == MIDDLE[0]:
                middle_h = keep.tile([P, MIDDLE[1] - MIDDLE[0], H], BF16, name="middle_h")
                for other in range(*MIDDLE):
                    h[other] = middle_h[:, other - MIDDLE[0], :]
            if e not in h:
                h[e] = keep.tile([P, H], BF16, name=f"h{e}")[:]
            nc.scalar.activation(
                out=sig[:].rearrange("c (u p d) -> c u p d", u=2, d=2),
                in_=a[:].rearrange("c (p u d) -> c u p d", u=2, d=2),
                func=SIGMOID,
            )
            nc.vector.tensor_tensor(
                out=h[e].rearrange("c (u p d) -> c u p d", u=2, d=2),
                in0=b[:].rearrange("c (p u d) -> c u p d", u=2, d=2),
                in1=sig[:].rearrange("c (u p d) -> c u p d", u=2, d=2),
                op=MULT,
            )

        def turn(first, last):
            count = last - first
            turned = bank("b" if count == 1 else "turned", [P, count, 2, C])
            for e in range(first, last):
                pairs = h[e].bitcast(F32)
                for u in range(2):
                    nc.tensor.transpose(turned[:, e - first, u, :], pairs[:, u * P : (u + 1) * P], ident[:])
            grouped[first] = keep.tile([P, count * C * 4], BF16, name=f"grouped{first}", align_bytes=64)
            copy = nc.vector.tensor_copy if first == E - 2 else nc.scalar.copy
            copy(
                out=grouped[first][:].bitcast(F32).rearrange("p (e c u) -> p e c u", e=count, u=2),
                in_=turned[:].rearrange("p e u c -> p e c u"),
            )

        gather(xw[:], U32, WORD_PIECES[:GATHER_DEPTH], slot_words, "slot_words")
        gather(xs[:, 0, :], U8, SCALE_PIECES, slot_scales, "slot_scales")
        for e in range(E):
            first_layer(e)
            if e == WORD_PIECES[0][1] - 1:
                gather(xw[:], U32, WORD_PIECES[GATHER_DEPTH:], slot_words, "slot_words")
            if e == TURN_GROUPS[1][1] - 1:
                turn(*TURN_GROUPS[0])
        for group in TURN_GROUPS[1:]:
            turn(*group)

        h_codes = keep.tile([P, S], U32, name="last_sig_then_codes", align_bytes=64)
        h_scales = keep.tile([P, S], U8, name="h_scales", align_bytes=64)
        for first, last in TURN_GROUPS:
            slots = slice(first * C, last * C)
            nc.vector.quantize_mx(out=h_codes[:, slots].bitcast(FP8X4), scales=h_scales[:, slots], in_=grouped[first][:])

        def second_layer(first, last, m, copy):
            acc = bank("a", [P, (last - first) * C])
            for e in range(first, last):
                slots = slice(e * C, (e + 1) * C)
                nc.tensor.matmul_mx(
                    out=acc[:, (e - first) * C : (e - first + 1) * C],
                    lhsT=expert_words(w2w, W2_CHUNKS, e)[:, 2 * P * m : 2 * P * (m + 1)].bitcast(FP4X4),
                    lhsT_scale=w2s[:, e, P * m : P * (m + 1)],
                    rhs=h_codes[:, slots].bitcast(FP8X4),
                    rhs_scale=h_scales[:, slots],
                    start=True,
                    stop=True,
                )
            copy(y[m][:, first * C : last * C], acc[:])

        second_layer(0, 4, 0, nc.scalar.copy)
        second_layer(4, 6, 0, nc.scalar.copy)
        second_layer(6, 8, 0, nc.vector.tensor_copy)
        second_layer(0, 4, 1, nc.scalar.copy)
        second_layer(4, 8, 1, nc.scalar.copy)

        for lo in (0, HALF):
            entries = slice(lo // PER_COLUMN, (lo + HALF) // PER_COLUMN)
            blocks = range(HALF // P)
            gated = []
            for j in range(2):
                fetched = keep.tile([P, HALF], F32, name=f"fetched{j}_{lo}")
                nc.vector.tensor_copy(fetched[:], y[0][:].indirect(pos_sb[j][:, entries]))
                by_token = bank("turned" if lo == 0 else "a", [P, HALF])
                for blk in blocks:
                    cols = slice(blk * P, (blk + 1) * P)
                    nc.tensor.transpose(by_token[:, cols], fetched[:, cols], ident[:])
                gated.append(keep.tile([P, HALF], F32, name=f"gated{j}_{lo}"))
                for blk in blocks:
                    cols = slice(blk * P, (blk + 1) * P)
                    token_block = lo // P + blk
                    scale = gate_cols[j][:, token_block : token_block + 1]
                    nc.scalar.activation(out=gated[j][:, cols], in_=by_token[:, cols], func=COPY, scale=scale)
            summed = bank("b", [P, HALF])
            for blk in blocks:
                cols = slice(blk * P, (blk + 1) * P)
                for j in range(2):
                    nc.tensor.matmul(
                        summed[:, cols],
                        lhsT=gated[j][:, cols],
                        rhs=ident[:],
                        start=(j == 0),
                        stop=(j == 1),
                        is_transpose=True,
                    )
            total = keep.tile([P, HALF], F32, name=f"total0_{lo}")
            nc.scalar.copy(total[:], summed[:])
            nc.sync.dma_start(out=out[0:P, lo : lo + HALF], in_=total[:])

        parts = [keep.tile([P, T], F32, name=f"part{j}") for j in range(2)]
        for j, lo, hi in ((0, 0, T), (1, 0, HALF), (1, HALF, T)):
            entries = slice(lo // PER_COLUMN, hi // PER_COLUMN)
            nc.vector.tensor_tensor(
                parts[j][:, lo:hi], y[1][:].indirect(pos_sb[j][:, entries]), gate_rows[j][:, lo:hi], MULT
            )
        for lo in (0, HALF):
            total = keep.tile([P, HALF], F32, name=f"total1_{lo}")
            nc.vector.tensor_tensor(total[:], parts[0][:, lo : lo + HALF], parts[1][:, lo : lo + HALF], ADD)
            nc.sync.dma_start(out=out[P : 2 * P, lo : lo + HALF], in_=total[:])
